import numpy as np
import ml_dtypes


def mxq(x, axis, fmt="e4m3"):
    dtype, down = {"e4m3": (ml_dtypes.float8_e4m3fn, 7), "e5m2": (ml_dtypes.float8_e5m2, 14)}[fmt]
    v = np.moveaxis(np.asarray(x, np.float32).astype(ml_dtypes.bfloat16).astype(np.float64), axis, -1)
    blocks = v.reshape(v.shape[:-1] + (-1, 32))
    amax = np.abs(blocks).max(-1, keepdims=True)
    byte = np.maximum(np.where(amax > 0, np.frexp(amax)[1] - 1 + 127, 0) - down, 1)
    scale = np.exp2(byte - 127.0)
    codes = (blocks / scale).astype(np.float32).astype(dtype).astype(np.float64)
    return np.moveaxis((codes * scale).reshape(v.shape), -1, axis)


WIDE = False


def mx_kscale(k):
    if not WIDE:
        return np.ones(k)
    levels = np.array([10, -10, 5, -5, 0])
    if k % 512:
        return np.exp2(np.random.permutation(np.resize(levels, k // 32))).repeat(32)
    a = np.empty((k // 512, 16))
    for p in range(k // 512):
        a[p, :8] = np.random.permutation(np.resize(levels, 8))
        for g in range(8):
            far = levels[np.abs(levels - a[p, g]) >= 10]
            a[p, g + 8] = far[np.random.randint(len(far))]
    return np.exp2(a.ravel()).repeat(32)


BF16 = ml_dtypes.bfloat16


def bf(x):
    return np.asarray(x, np.float32).astype(BF16)


def f64(x):
    return np.asarray(x).astype(np.float64)


B, D, T, P, Q = 8, 512, 512, 512, 512


def scaled_softmax(e):
    p = np.exp(e - e.max(axis=-1, keepdims=True))
    return e.shape[-1] * (p / p.sum(axis=-1, keepdims=True))


def draw0():
    s, t = mx_kscale(D), mx_kscale(T)
    return {
        "x": bf(np.random.standard_normal((B, D, T)) * s[None, :, None]),
        "w1": bf(np.random.standard_normal((P, D)) / np.sqrt(D) / s[None, :]),
        "g": bf((1.0 + 0.1 * np.random.standard_normal(T)) * t),
        "w": bf(np.random.standard_normal((T, Q)) / np.sqrt(T) / t[:, None]),
        "w2": bf(np.random.standard_normal((T, Q)) / np.sqrt(T) / t[:, None]),
        "lam": bf(np.random.uniform(0.3, 0.7, P)),
        "bias": bf(0.4 * np.random.standard_normal((P, Q))),
    }


def core(x, w1, g, w, w2, lam, bias):
    h0 = mxq(f64(w1), 1, "e4m3") @ mxq(f64(x), 1, "e4m3")
    h = h0 * f64(g)[None, None, :]
    hq = mxq(h, 2, "e4m3")
    u = hq @ mxq(f64(w2), 0, "e4m3")
    e = hq @ mxq(f64(w), 0, "e4m3")
    a = scaled_softmax(e)
    mix = f64(lam)[None, :, None]
    z = mix * u * a + (1.0 - mix) * u + f64(bias)[None, :, :]
    return np.tanh(z)


def e4m3fn_bytes(y):
    return np.clip(np.asarray(y, np.float64), -448.0, 448.0).astype(np.float32).astype(ml_dtypes.float8_e4m3fn).view(np.uint8)


def e4m3fn_values(b):
    return np.asarray(b, np.uint8).view(ml_dtypes.float8_e4m3fn).astype(np.float64)


def setup_inputs():
    d = draw0()
    x0 = np.asarray(d['x']).astype(np.float64)
    s = (np.max(np.abs(x0), axis=(0, 2), keepdims=True) / 448.0).astype(np.float32)
    out = {}
    for k, v in d.items():
        if k == 'x':
            out['x_bytes'] = e4m3fn_bytes(x0 / s.astype(np.float64))
            out['x_scale'] = s
        else:
            out[k] = v
    return out


def reference(x_bytes, x_scale, w1, g, w, w2, lam, bias):
    return core(e4m3fn_values(x_bytes) * x_scale.astype(np.float64), w1, g, w, w2, lam, bias)

@@ -1,0 +1,406 @@
+from contextlib import ExitStack
+
+import concourse.mybir as mybir
+from concourse.masks import make_identity
+
+F32 = mybir.dt.float32
+BF16 = mybir.dt.bfloat16
+U32 = mybir.dt.uint32
+U8 = mybir.dt.uint8
+FP8 = mybir.dt.float8_e4m3fn
+FP8X4 = mybir.dt.float8_e4m3fn_x4
+ALU = mybir.AluOpType
+ACT = mybir.ActivationFunctionType
+AX = mybir.AxisListType
+
+NB, N, P, J = 8, 512, 128, 4
+NT = NB * J
+FLOPS = 6 * NB * N * N * N
+EPS = 1e-12
+
+PEZ = 19
+XINT = 'G'
+HB = 1
+DEQV = 0
+PX1 = 'VVGG'
+
+
+def tile_temporalaugmentedbilinear_kernel(tc, x_bytes, x_scale, w1, g, w, w2, lam, bias, out):
+    nc = tc.nc
+    pez = set(i for i in range(2, NT - 2) if (i * PEZ) // NT != ((i + 1) * PEZ) // NT)
+    with ExitStack() as ctx:
+        keep = ctx.enter_context(tc.tile_pool(name="keep", bufs=1))
+        xpool = ctx.enter_context(tc.tile_pool(name="xpool", bufs=2))
+        ep = ctx.enter_context(tc.tile_pool(name="ep", bufs=3))
+        st = ctx.enter_context(tc.tile_pool(name="st", bufs=6))
+        ps = ctx.enter_context(tc.psum_pool(name="ps", bufs=2))
+        hbufs = 2 if PEZ else 4
+
+        ctx.enter_context(tc.manual_schedule())
+
+        xs4 = keep.tile([P, J], F32, name="xs4")
+        nc.sync.dma_start(out=xs4[:], in_=x_scale.rearrange("o (p j) e -> p (o j e)", j=J))
+        xb = {}
+
+        def load_x(b):
+            t = keep.tile([P, J, N], U8, name="xb%d" % b, align_bytes=64)
+            xb[b] = t
+            nc.sync.dma_start(out=t[:], in_=x_bytes[b].rearrange("(p j) t -> p j t", j=J))
+
+        load_x(0)
+        w1_sb = keep.tile([P, J * N], BF16, name="w1_sb", align_bytes=64)
+        nc.sync.dma_start(out=w1_sb[:], in_=w1.rearrange("(m c) d -> m (c d)", c=J))
+        g_bf = keep.tile([P, J], BF16, name="g_bf")
+        nc.sync.dma_start(out=g_bf[:], in_=g.rearrange("(p j) -> p j", j=J))
+        w_sb = keep.tile([P, J, N], BF16, name="w_sb", align_bytes=64)
+        nc.sync.dma_start(out=w_sb[:], in_=w.rearrange("(p j) q -> p j q", j=J))
+        w2_sb = keep.tile([P, J, N], BF16, name="w2_sb", align_bytes=64)
+        nc.sync.dma_start(out=w2_sb[:], in_=w2.rearrange("(p j) q -> p j q", j=J))
+        load_x(1)
+        lam_bf = keep.tile([P, J], BF16, name="lam_bf")
+        nc.sync.dma_start(out=lam_bf[:], in_=lam.rearrange("(m c) -> m c", c=J))
+        bias_sb = keep.tile([P, J, N], BF16, name="bias_sb", align_bytes=64)
+        nc.sync.dma_start(out=bias_sb[:], in_=bias.rearrange("(m c) q -> m c q", c=J))
+        for b in range(2, NB):
+            load_x(b)
+
+        warm = keep.tile([P, 1], F32, name="warm")
+        nc.vector.memset(warm[:], 0.0)
+        nc.scalar.activation(out=warm[:], in_=warm[:], func=ACT.Exp)
+        ident = keep.tile([P, P], F32, name="ident")
+        make_identity(nc, ident[:])
+        if PEZ:
+            ident_bf = keep.tile([P, P], BF16, name="ident_bf")
+            nc.gpsimd.tensor_copy(out=ident_bf[:], in_=ident[:])
+        g_f = keep.tile([P, J], F32, name="g_f")
+        nc.gpsimd.tensor_copy(out=g_f[:], in_=g_bf[:])
+
+        wq = {}
+        for nm in ("w1", "w", "w2"):
+            wq[nm] = (
+                keep.tile([P, N * J], BF16, name=nm + "_g", align_bytes=64),
+                keep.tile([P, N], U32, name=nm + "_c", align_bytes=64),
+                keep.tile([P, N], U8, name=nm + "_s", align_bytes=64),
+            )
+
+        def quant(codes, scales, src, lo, hi):
+            nc.vector.quantize_mx(out=codes[:, lo:hi].bitcast(FP8X4), scales=scales[:, lo:hi], in_=src[:, J * lo : J * hi])
+
+        def quant_w(nm):
+            gr, codes, scales = wq[nm]
+            quant(codes, scales, gr, 0, N)
+
+        def eng_copy(e, out, in_):
+            if e == "V":
+                nc.vector.tensor_copy(out=out, in_=in_)
+            elif e == "S":
+                nc.scalar.copy(out=out, in_=in_)
+            else:
+                nc.gpsimd.tensor_scalar(out=out, in0=in_, scalar1=1.0, scalar2=0.0, op0=ALU.mult, op1=ALU.add)
+
+        def w_inter(nm, src, e, lo, hi):
+            gr = wq[nm][0]
+            eng_copy(
+                e,
+                gr[:, J * lo : J * hi].rearrange("p (q j) -> p q j", j=J),
+                src[:, :, lo:hi].rearrange("p j q -> p q j"),
+            )
+
+        xp, xg, xc, xsc = {}, {}, {}, {}
+
+        def deq(b, j, e):
+            if b >= NB:
+                return
+            if b not in xp:
+                xp[b] = xpool.tile([P, J, N], BF16, name="xp", align_bytes=64)
+            src = xb[b][:, j, :].bitcast(FP8)
+            if e == "V":
+                nc.vector.tensor_scalar(out=xp[b][:, j, :], in0=src, scalar1=xs4[:, j : j + 1], scalar2=None, op0=ALU.mult)
+            else:
+                nc.scalar.activation(out=xp[b][:, j, :], in_=src, func=ACT.Copy, scale=xs4[:, j : j + 1])
+
+        def x_inter(b, jj, e):
+            if b >= NB:
+                return
+            if b not in xg:
+                xg[b] = xpool.tile([P, N * J], BF16, name="xg", align_bytes=64)
+            a = jj * P * J
+            eng_copy(
+                e,
+                xg[b][:, a : a + P * J].rearrange("p (m j) -> p m j", j=J),
+                xp[b][:].rearrange("p j (m t) -> p t m j", t=J)[:, jj],
+            )
+
+        def quant_x(b):
+            if b >= NB:
+                return
+            xc[b] = xpool.tile([P, N], U32, name="xc", align_bytes=64)
+            xsc[b] = xpool.tile([P, N], U8, name="xsc", align_bytes=64)
+            quant(xc[b], xsc[b], xg[b], 0, N)
+
+        hg, hc, hs, hp, hpl = {}, {}, {}, {}, {}
+
+        def h_tiles(b):
+            if b not in hg:
+                hg[b] = xpool.tile([P, N * J], BF16, name="hg", align_bytes=64)
+                hc[b] = xpool.tile([P, N], U32, name="hc", align_bytes=64)
+                hs[b] = xpool.tile([P, N], U8, name="hs", align_bytes=64)
+
+        def mx(out_ap, lc, ls, rc, rs):
+            nc.tensor.matmul_mx(out=out_ap, lhsT=lc.bitcast(FP8X4), lhsT_scale=ls, rhs=rc.bitcast(FP8X4), rhs_scale=rs, start=True, stop=True)
+
+        def mm_hA(b, c):
+            if b >= NB:
+                return
+            t = ps.tile([P, J, P], F32, name="hps", tag="h", bufs=hbufs)
+            hp[(b, c)] = t
+            wc_, ws_ = wq["w1"][1], wq["w1"][2]
+            for jj in range(J):
+                s = slice(jj * P, (jj + 1) * P)
+                r = slice(c * P, (c + 1) * P)
+                mx(t[:, jj, :], xc[b][:, s], xsc[b][:, s], wc_[:, r], ws_[:, r])
+
+        def evacA(b, c):
+            if b >= NB:
+                return
+            h_tiles(b)
+            nc.vector.tensor_tensor(
+                out=hg[b][:, c * P * J : (c + 1) * P * J].rearrange("p (n j) -> p n j", j=J),
+                in0=hp[(b, c)][:].rearrange("p j n -> p n j"),
+                in1=g_bf[:].unsqueeze(1).to_broadcast([P, P, J]),
+                op=ALU.mult,
+            )
+
+        def mm_hB(b, half):
+            if b >= NB:
+                return
+            t = ps.tile([P, 2, 2 * P], F32, name="hpb", tag="h", bufs=hbufs)
+            hp[(b, "B", half)] = t
+            wc_, ws_ = wq["w1"][1], wq["w1"][2]
+            for k in range(2):
+                jj = 2 * half + k
+                s = slice(jj * P, (jj + 1) * P)
+                r = slice(2 * P, 4 * P)
+                mx(t[:, k, :], xc[b][:, s], xsc[b][:, s], wc_[:, r], ws_[:, r])
+
+        def evacB(b, jj):
+            if b >= NB:
+                return
+            h_tiles(b)
+            if b not in hpl:
+                hpl[b] = xpool.tile([P, J, 2 * P], BF16, name="hpl", align_bytes=64)
+            nc.scalar.activation(out=hpl[b][:, jj, :], in_=hp[(b, "B", jj // 2)][:, jj % 2, :], func=ACT.Copy, scale=g_f[:, jj : jj + 1])
+
+        def interB(b, part, e):
+            if b >= NB:
+                return
+            a = (2 + part) * P * J
+            eng_copy(
+                e,
+                hg[b][:, a : a + P * J].rearrange("p (n j) -> p n j", j=J),
+                hpl[b][:, :, part * P : (part + 1) * P].rearrange("p j n -> p n j"),
+            )
+
+        def quant_h(b, lo, hi):
+            if b >= NB:
+                return
+            quant(hc[b], hs[b], hg[b], lo * P, hi * P)
+
+        e_ps, u_ps, z_ps, E, G, Z = {}, {}, {}, {}, {}, {}
+        nmax, ssum, rr, rec, cc, dg = {}, {}, {}, {}, {}, {}
+
+        def mm2(i, nm, store, tag):
+            if i >= NT:
+                return
+            b, c = divmod(i, J)
+            t = ps.tile([P, N], F32, name=tag + "ps", tag=tag, bufs=2)
+            store[i] = t
+            s = slice(c * P, (c + 1) * P)
+            mx(t[:], hc[b][:, s], hs[b][:, s], wq[nm][1][:], wq[nm][2][:])
+
+        def mm_e(i):
+            mm2(i, "w", e_ps, "e")
+
+        def mm_u(i):
+            mm2(i, "w2", u_ps, "u")
+
+        def rowmax(i):
+            if i >= NT:
+                return
+            nmax[i] = st.tile([P, 1], F32, name="nmax")
+            nc.vector.tensor_reduce(out=nmax[i][:], in_=e_ps[i][:], axis=AX.X, op=ALU.max, negate=True)
+
+        def expo(i):
+            if i >= NT:
+                return
+            E[i] = ep.tile([P, N], F32, name="E")
+            ssum[i] = st.tile([P, 1], F32, name="ssum")
+            nc.scalar.activation(out=E[i][:], in_=e_ps[i][:], func=ACT.Exp, bias=nmax[i][:], accum_out=ssum[i][:])
+
+        def small(i):
+            if i >= NT:
+                return
+            c = i % J
+            rr[i] = st.tile([P, 1], F32, name="rr")
+            nc.gpsimd.tensor_tensor(out=rr[i][:], in0=ssum[i][:], in1=kk[:, c : c + 1], op=ALU.mult)
+
+        def small2(i):
+            if i >= NT:
+                return
+            c = i % J
+            rec[i] = st.tile([P, 1], F32, name="rec")
+            nc.vector.reciprocal(out=rec[i][:], in_=ssum[i][:])
+            if i in pez:
+                dg[i] = st.tile([P, P], F32, name="dg")
+                nc.gpsimd.tensor_scalar(out=dg[i][:], in0=ident[:], scalar1=rec[i][:], scalar2=L[:, c : c + 1], op0=ALU.mult, op1=ALU.mult)
+            else:
+                cc[i] = st.tile([P, 1], F32, name="cc")
+                nc.gpsimd.tensor_tensor(out=cc[i][:], in0=rec[i][:], in1=L[:, c : c + 1], op=ALU.mult)
+
+        def gate(i):
+            G[i] = ep.tile([P, N], F32, name="G")
+            nc.vector.scalar_tensor_tensor(out=G[i][:], in0=E[i][:], scalar=rr[i][:], in1=u_ps[i][:], op0=ALU.add, op1=ALU.mult)
+
+        def mix(i):
+            c = i % J
+            if i in pez:
+                t = ps.tile([P, N], F32, name="zps", tag="z", bufs=2)
+                z_ps[i] = t
+                nc.tensor.matmul(t[:], lhsT=ident_bf[:], rhs=bias_sb[:, c, :], start=True, stop=False)
+                nc.tensor.matmul(t[:], lhsT=dg[i][:], rhs=G[i][:], start=False, stop=True)
+            else:
+                Z[i] = ep.tile([P, N], F32, name="Z")
+                nc.vector.scalar_tensor_tensor(out=Z[i][:], in0=G[i][:], scalar=cc[i][:], in1=bias_sb[:, c, :], op0=ALU.mult, op1=ALU.add)
+
+        def final(i):
+            if i < 0:
+                return
+            b, c = divmod(i, J)
+            o = ep.tile([P, N], F32, name="O")
+            src = z_ps[i] if i in pez else Z[i]
+            nc.scalar.activation(out=o[:], in_=src[:], func=ACT.Tanh)
+            nc.sync.dma_start(out=out[b].rearrange("(m c) q -> m c q", c=J)[:, c, :], in_=o[:])
+
+        deq(0, 0, "V")
+        deq(0, 3, "S")
+        deq(0, 1, "V")
+        deq(0, 2, "V")
+        for jj in range(J):
+            x_inter(0, jj, "V")
+        words = w1_sb[:].bitcast(F32)
+        w1g_words = wq["w1"][0][:].bitcast(F32)
+        for half in range(2):
+            t = ps.tile([P, 2, 2, P], F32, name="w1t", tag="h", bufs=hbufs)
+            for k in range(2):
+                c = 2 * half + k
+                for u in range(2):
+                    nc.tensor.transpose(t[:, k, u, :], words[:, 256 * c + u : 256 * (c + 1) : 2], ident[:])
+            o = w1g_words[:, 512 * half : 512 * (half + 1)].rearrange("p (c m u) -> p c m u", c=2, u=2)
+            i_ = t[:].rearrange("p c u m -> p c m u")
+            nc.scalar.copy(out=o, in_=i_)
+        quant_x(0)
+        quant_w("w1")
+        for q in range(4):
+            w_inter("w", w_sb, "G", 128 * q, 128 * (q + 1))
+        mm_hA(0, 0)
+        mm_hA(0, 1)
+        evacA(0, 0)
+        evacA(0, 1)
+        quant_h(0, 0, 1)
+        quant_w("w")
+        mm_e(0)
+        mm_hA(0, 2)
+        mm_hA(0, 3)
+        for q in range(4):
+            w_inter("w2", w2_sb, "S", 128 * q, 128 * (q + 1))
+        quant_h(0, 1, 2)
+        rowmax(0)
+        expo(0)
+        quant_w("w2")
+        mm_u(0)
+        mm_e(1)
+        L = keep.tile([P, J], F32, name="L")
+        nc.vector.tensor_scalar(out=L[:], in0=lam_bf[:], scalar1=float(N), scalar2=EPS, op0=ALU.mult, op1=ALU.add)
+        rl = keep.tile([P, J], F32, name="rl")
+        nc.vector.reciprocal(out=rl[:], in_=L[:])
+        dd = keep.tile([P, J], F32, name="dd")
+        nc.gpsimd.tensor_scalar(out=dd[:], in0=lam_bf[:], scalar1=-1.0, scalar2=1.0, op0=ALU.mult, op1=ALU.add)
+        kk = keep.tile([P, J], F32, name="kk")
+        nc.gpsimd.tensor_tensor(out=kk[:], in0=dd[:], in1=rl[:], op=ALU.mult)
+        small(0)
+        small2(0)
+        evacA(0, 2)
+        evacA(0, 3)
+        quant_h(0, 2, 4)
+        for j in range(J):
+            deq(1, j, "S")
+        for jj in range(J):
+            x_inter(1, jj, PX1[jj])
+        deq(2, 0, "S")
+        deq(2, 1, "S")
+
+        for i in range(NT):
+            b, s = divmod(i, J)
+            if s == 0:
+                deq(b + 2, 2, "S")
+                deq(b + 2, 3, "V" if DEQV else "S")
+            if s == 3:
+                deq(b + 3, 0, "S")
+                deq(b + 3, 1, "V" if DEQV > 1 else "S")
+            if HB:
+                if s == 1:
+                    evacB(b + 1, 0)
+                    evacB(b + 1, 1)
+                if s == 2:
+                    evacB(b + 1, 2)
+                    evacB(b + 1, 3)
+            rowmax(i + 1)
+            if s == 0:
+                quant_x(b + 1)
+            expo(i + 1)
+            small(i + 1)
+            mm_u(i + 1)
+            gate(i)
+            if HB:
+                if s == 0:
+                    mm_hA(b + 1, 0)
+                    mm_hB(b + 1, 0)
+                    if b > 0:
+                        quant_h(b, 2, 4)
+                if s == 1:
+                    evacA(b + 1, 0)
+                    mm_hA(b + 1, 1)
+                    mm_hB(b + 1, 1)
+                if s == 2:
+                    quant_h(b + 1, 0, 1)
+                    evacA(b + 1, 1)
+                if s == 3:
+                    quant_h(b + 1, 1, 2)
+                    interB(b + 1, 0, "G")
+                    interB(b + 1, 1, "G")
+            else:
+                if s == 0:
+                    mm_hA(b + 1, 0)
+                    mm_hA(b + 1, 1)
+                if s == 1:
+                    evacA(b + 1, 0)
+                    evacA(b + 1, 1)
+                    mm_hA(b + 1, 2)
+                    mm_hA(b + 1, 3)
+                if s == 2:
+                    quant_h(b + 1, 0, 2)
+                    evacA(b + 1, 2)
+                if s == 3:
+                    evacA(b + 1, 3)
+                    quant_h(b + 1, 2, 4)
+            if s == 1:
+                x_inter(b + 2, 0, XINT)
+                x_inter(b + 2, 1, XINT)
+            if s == 2:
+                x_inter(b + 2, 2, XINT)
+                x_inter(b + 2, 3, XINT)
+            mm_e(i + 2)
+            mix(i)
+            small2(i + 1)
+            final(i - 1)
+        final(NT - 1)

@@ -19,10 +19,17 @@ FLOPS = 6 * NB * N * N * N
 EPS = 1e-12
 
 PEZ = 19
-XINT = 'G'
+XINT = 'VVVS'
 HB = 1
 DEQV = 0
-PX1 = 'VVGG'
+PX1 = 'VVVV'
+RENG = 'S'
+CENG = 'V'
+BINT = 'VV'
+WENG = 'SSSS'
+W2ENG = 'SSSS'
+EB = "SSSS"
+PD2 = "SSSS"
 
 
 def tile_temporalaugmentedbilinear_kernel(tc, x_bytes, x_scale, w1, g, w, w2, lam, bias, out):
@@ -138,6 +145,12 @@ def tile_temporalaugmentedbilinear_kernel(tc, x_bytes, x_scale, w1, g, w, w2, la
             xsc[b] = xpool.tile([P, N], U8, name="xsc", align_bytes=64)
             quant(xc[b], xsc[b], xg[b], 0, N)
 
+        def quant_xp(b, jj):
+            if b not in xc:
+                xc[b] = xpool.tile([P, N], U32, name="xc", align_bytes=64)
+                xsc[b] = xpool.tile([P, N], U8, name="xsc", align_bytes=64)
+            quant(xc[b], xsc[b], xg[b], jj * P, (jj + 1) * P)
+
         hg, hc, hs, hp, hpl = {}, {}, {}, {}, {}
 
         def h_tiles(b):
@@ -242,7 +255,11 @@ def tile_temporalaugmentedbilinear_kernel(tc, x_bytes, x_scale, w1, g, w, w2, la
                 return
             c = i % J
             rr[i] = st.tile([P, 1], F32, name="rr")
-            nc.gpsimd.tensor_tensor(out=rr[i][:], in0=ssum[i][:], in1=kk[:, c : c + 1], op=ALU.mult)
+            if RENG == "S":
+                nc.scalar.activation(out=rr[i][:], in_=ssum[i][:], func=ACT.Copy, scale=kk[:, c : c + 1])
+            else:
+                e = nc.gpsimd if RENG == "G" else nc.vector
+                e.tensor_tensor(out=rr[i][:], in0=ssum[i][:], in1=kk[:, c : c + 1], op=ALU.mult)
 
         def small2(i):
             if i >= NT:
@@ -255,13 +272,16 @@ def tile_temporalaugmentedbilinear_kernel(tc, x_bytes, x_scale, w1, g, w, w2, la
                 nc.gpsimd.tensor_scalar(out=dg[i][:], in0=ident[:], scalar1=rec[i][:], scalar2=L[:, c : c + 1], op0=ALU.mult, op1=ALU.mult)
             else:
                 cc[i] = st.tile([P, 1], F32, name="cc")
-                nc.gpsimd.tensor_tensor(out=cc[i][:], in0=rec[i][:], in1=L[:, c : c + 1], op=ALU.mult)
+                e = nc.gpsimd if CENG == "G" else nc.vector
+                e.tensor_tensor(out=cc[i][:], in0=rec[i][:], in1=L[:, c : c + 1], op=ALU.mult)
 
         def gate(i):
             G[i] = ep.tile([P, N], F32, name="G")
             nc.vector.scalar_tensor_tensor(out=G[i][:], in0=E[i][:], scalar=rr[i][:], in1=u_ps[i][:], op0=ALU.add, op1=ALU.mult)
 
         def mix(i):
+            if i < 0:
+                return
             c = i % J
             if i in pez:
                 t = ps.tile([P, N], F32, name="zps", tag="z", bufs=2)
@@ -281,44 +301,57 @@ def tile_temporalaugmentedbilinear_kernel(tc, x_bytes, x_scale, w1, g, w, w2, la
             nc.scalar.activation(out=o[:], in_=src[:], func=ACT.Tanh)
             nc.sync.dma_start(out=out[b].rearrange("(m c) q -> m c q", c=J)[:, c, :], in_=o[:])
 
+        def w1_part(c, e):
+            t = ps.tile([P, 2, P], F32, name="w1t", tag="h", bufs=hbufs)
+            for u in range(2):
+                nc.tensor.transpose(t[:, u, :], words[:, 256 * c + u : 256 * (c + 1) : 2], ident[:])
+            o = w1g_words[:, 256 * c : 256 * (c + 1)].rearrange("p (m u) -> p m u", u=2)
+            i_ = t[:].rearrange("p u m -> p m u")
+            if e == "S":
+                nc.scalar.copy(out=o, in_=i_)
+            else:
+                nc.vector.tensor_copy(out=o, in_=i_)
+
+        words = w1_sb[:].bitcast(F32)
+        w1g_words = wq["w1"][0][:].bitcast(F32)
         deq(0, 0, "V")
         deq(0, 3, "S")
         deq(0, 1, "V")
         deq(0, 2, "V")
-        for jj in range(J):
-            x_inter(0, jj, "V")
-        words = w1_sb[:].bitcast(F32)
-        w1g_words = wq["w1"][0][:].bitcast(F32)
-        for half in range(2):
-            t = ps.tile([P, 2, 2, P], F32, name="w1t", tag="h", bufs=hbufs)
-            for k in range(2):
-                c = 2 * half + k
-                for u in range(2):
-                    nc.tensor.transpose(t[:, k, u, :], words[:, 256 * c + u : 256 * (c + 1) : 2], ident[:])
-            o = w1g_words[:, 512 * half : 512 * (half + 1)].rearrange("p (c m u) -> p c m u", c=2, u=2)
-            i_ = t[:].rearrange("p c u m -> p c m u")
-            nc.scalar.copy(out=o, in_=i_)
-        quant_x(0)
-        quant_w("w1")
-        for q in range(4):
-            w_inter("w", w_sb, "G", 128 * q, 128 * (q + 1))
+        for c in range(4):
+            w1_part(c, "S")
+        x_inter(0, 0, "V")
+        x_inter(0, 1, "V")
+        quant_xp(0, 0)
+        x_inter(0, 2, "V")
+        quant_xp(0, 1)
+        x_inter(0, 3, "V")
+        quant_xp(0, 2)
+        quant(wq["w1"][1], wq["w1"][2], wq["w1"][0], 0, P)
+        quant_xp(0, 3)
         mm_hA(0, 0)
+        quant(wq["w1"][1], wq["w1"][2], wq["w1"][0], P, 2 * P)
+        quant(wq["w1"][1], wq["w1"][2], wq["w1"][0], 2 * P, N)
         mm_hA(0, 1)
+        for q in range(4):
+            w_inter("w", w_sb, WENG[q], 128 * q, 128 * (q + 1))
+        for q in range(4):
+            w_inter("w2", w2_sb, W2ENG[q], 128 * q, 128 * (q + 1))
+        deq(1, 0, "V")
+        deq(1, 1, "V")
         evacA(0, 0)
         evacA(0, 1)
-        quant_h(0, 0, 1)
-        quant_w("w")
-        mm_e(0)
         mm_hA(0, 2)
         mm_hA(0, 3)
-        for q in range(4):
-            w_inter("w2", w2_sb, "S", 128 * q, 128 * (q + 1))
+        quant_w("w")
+        quant_h(0, 0, 1)
+        mm_e(0)
         quant_h(0, 1, 2)
+        mm_e(1)
+        deq(1, 2, "V")
+        deq(1, 3, "V")
         rowmax(0)
         expo(0)
-        quant_w("w2")
-        mm_u(0)
-        mm_e(1)
         L = keep.tile([P, J], F32, name="L")
         nc.vector.tensor_scalar(out=L[:], in0=lam_bf[:], scalar1=float(N), scalar2=EPS, op0=ALU.mult, op1=ALU.add)
         rl = keep.tile([P, J], F32, name="rl")
@@ -327,80 +360,78 @@ def tile_temporalaugmentedbilinear_kernel(tc, x_bytes, x_scale, w1, g, w, w2, la
         nc.gpsimd.tensor_scalar(out=dd[:], in0=lam_bf[:], scalar1=-1.0, scalar2=1.0, op0=ALU.mult, op1=ALU.add)
         kk = keep.tile([P, J], F32, name="kk")
         nc.gpsimd.tensor_tensor(out=kk[:], in0=dd[:], in1=rl[:], op=ALU.mult)
-        small(0)
-        small2(0)
         evacA(0, 2)
         evacA(0, 3)
+        quant_w("w2")
+        mm_u(0)
         quant_h(0, 2, 4)
-        for j in range(J):
-            deq(1, j, "S")
+        small(0)
         for jj in range(J):
             x_inter(1, jj, PX1[jj])
-        deq(2, 0, "S")
-        deq(2, 1, "S")
+        for j in range(J):
+            deq(2, j, PD2[j])
+        if PX1 == "VVVV":
+            quant_x(1)
 
         for i in range(NT):
             b, s = divmod(i, J)
-            if s == 0:
-                deq(b + 2, 2, "S")
-                deq(b + 2, 3, "V" if DEQV else "S")
-            if s == 3:
-                deq(b + 3, 0, "S")
-                deq(b + 3, 1, "V" if DEQV > 1 else "S")
-            if HB:
-                if s == 1:
-                    evacB(b + 1, 0)
-                    evacB(b + 1, 1)
-                if s == 2:
-                    evacB(b + 1, 2)
-                    evacB(b + 1, 3)
+            nb = b + 1
+            mm_u(i + 1)
             rowmax(i + 1)
+            small2(i)
+            gate(i)
             if s == 0:
-                quant_x(b + 1)
+                if b == 0 and PX1 != "VVVV":
+                    quant_x(1)
+                mm_hA(nb, 0)
+                if HB:
+                    mm_hB(nb, 0)
+            if s == 1:
+                quant_h(nb, 0, 1)
+                mm_hA(nb, 1)
+                if HB:
+                    mm_hB(nb, 1)
+                else:
+                    mm_hA(nb, 2)
+            if s == 2:
+                quant_h(nb, 1, 2)
+                if not HB:
+                    mm_hA(nb, 3)
+                deq(b + 3, 0, "S")
+            if s == 3:
+                deq(b + 3, 2, "S")
+            mm_e(i + 2)
             expo(i + 1)
             small(i + 1)
-            mm_u(i + 1)
-            gate(i)
-            if HB:
-                if s == 0:
-                    mm_hA(b + 1, 0)
-                    mm_hB(b + 1, 0)
-                    if b > 0:
-                        quant_h(b, 2, 4)
-                if s == 1:
-                    evacA(b + 1, 0)
-                    mm_hA(b + 1, 1)
-                    mm_hB(b + 1, 1)
-                if s == 2:
-                    quant_h(b + 1, 0, 1)
-                    evacA(b + 1, 1)
-                if s == 3:
-                    quant_h(b + 1, 1, 2)
-                    interB(b + 1, 0, "G")
-                    interB(b + 1, 1, "G")
-            else:
-                if s == 0:
-                    mm_hA(b + 1, 0)
-                    mm_hA(b + 1, 1)
-                if s == 1:
-                    evacA(b + 1, 0)
-                    evacA(b + 1, 1)
-                    mm_hA(b + 1, 2)
-                    mm_hA(b + 1, 3)
-                if s == 2:
-                    quant_h(b + 1, 0, 2)
-                    evacA(b + 1, 2)
-                if s == 3:
-                    evacA(b + 1, 3)
-                    quant_h(b + 1, 2, 4)
+            mix(i - 1)
+            final(i - 2)
+            if s == 0:
+                evacA(nb, 0)
+                if HB:
+                    evacB(nb, 0)
+                    evacB(nb, 1)
+                x_inter(b + 2, 0, XINT[0])
+                x_inter(b + 2, 1, XINT[1])
             if s == 1:
-                x_inter(b + 2, 0, XINT)
-                x_inter(b + 2, 1, XINT)
+                evacA(nb, 1)
+                if HB:
+                    evacB(nb, 2)
+                    evacB(nb, 3)
+                x_inter(b + 2, 2, XINT[2])
+                x_inter(b + 2, 3, XINT[3])
             if s == 2:
-                x_inter(b + 2, 2, XINT)
-                x_inter(b + 2, 3, XINT)
-            mm_e(i + 2)
-            mix(i)
-            small2(i + 1)
-            final(i - 1)
+                deq(b + 3, 1, "V" if DEQV > 0 else "S")
+                if HB:
+                    interB(nb, 0, BINT[0])
+                    interB(nb, 1, BINT[1])
+                else:
+                    evacA(nb, 2)
+            if s == 3:
+                if not HB:
+                    evacA(nb, 3)
+                deq(b + 3, 3, "V" if DEQV > 1 else "S")
+                quant_h(nb, 2, 4)
+                quant_x(b + 2)
+        mix(NT - 1)
+        final(NT - 2)
         final(NT - 1)

@@ -18,13 +18,21 @@ NT = NB * J
 FLOPS = 6 * NB * N * N * N
 EPS = 1e-12
 
-PEZ = 19
-XINT = 'VVVS'
+PEZ = 1
+XINT = "VVVV"
 HB = 1
 DEQV = 0
-PX1 = 'VVVV'
-RENG = 'S'
-CENG = 'V'
+PD1 = "VVVV"
+PX = 'SSVV'
+XE = 'SVSV'
+DE = "SSSS"
+PEX = (6, 14, 22, 26)
+PEM = (1, 3)
+IBP = 0
+PX1 = "VVVV"
+RENG = 'G'
+REC = 'G'
+CENG = 'G'
 BINT = 'VV'
 WENG = 'SSSS'
 W2ENG = 'SSSS'
@@ -34,7 +42,7 @@ PD2 = "SSSS"
 
 def tile_temporalaugmentedbilinear_kernel(tc, x_bytes, x_scale, w1, g, w, w2, lam, bias, out):
     nc = tc.nc
-    pez = set(i for i in range(2, NT - 2) if (i * PEZ) // NT != ((i + 1) * PEZ) // NT)
+    pez = set(i for i in range(NT - 2) if PEZ and (i % 4 in PEM or i in PEX))
     with ExitStack() as ctx:
         keep = ctx.enter_context(tc.tile_pool(name="keep", bufs=1))
         xpool = ctx.enter_context(tc.tile_pool(name="xpool", bufs=2))
@@ -82,6 +90,10 @@ def tile_temporalaugmentedbilinear_kernel(tc, x_bytes, x_scale, w1, g, w, w2, la
         g_f = keep.tile([P, J], F32, name="g_f")
         nc.gpsimd.tensor_copy(out=g_f[:], in_=g_bf[:])
 
+        if REC != "V":
+            neg1 = keep.tile([P, 1], F32, name="neg1")
+            nc.gpsimd.memset(neg1[:], -1.0)
+
         wq = {}
         for nm in ("w1", "w", "w2"):
             wq[nm] = (
@@ -119,24 +131,29 @@ def tile_temporalaugmentedbilinear_kernel(tc, x_bytes, x_scale, w1, g, w, w2, la
             if b >= NB:
                 return
             if b not in xp:
-                xp[b] = xpool.tile([P, J, N], BF16, name="xp", align_bytes=64)
+                xp[b] = xpool.tile([P, J, N], BF16, name="xp", bufs=3, align_bytes=64)
             src = xb[b][:, j, :].bitcast(FP8)
             if e == "V":
                 nc.vector.tensor_scalar(out=xp[b][:, j, :], in0=src, scalar1=xs4[:, j : j + 1], scalar2=None, op0=ALU.mult)
             else:
                 nc.scalar.activation(out=xp[b][:, j, :], in_=src, func=ACT.Copy, scale=xs4[:, j : j + 1])
 
-        def x_inter(b, jj, e):
+        def x_inter(b, m0, m1, e):
             if b >= NB:
                 return
             if b not in xg:
                 xg[b] = xpool.tile([P, N * J], BF16, name="xg", align_bytes=64)
-            a = jj * P * J
-            eng_copy(
-                e,
-                xg[b][:, a : a + P * J].rearrange("p (m j) -> p m j", j=J),
-                xp[b][:].rearrange("p j (m t) -> p t m j", t=J)[:, jj],
-            )
+            if e == "V":
+                o = xg[b][:].rearrange("p (t a m j) -> p a t (m j)", t=J, a=P // 2, j=J)[:, m0 // 2 : m1 // 2]
+                i_ = xp[b][:].rearrange("p j (a m t) -> p a t m j", t=J, m=2)[:, m0 // 2 : m1 // 2]
+                o = o.rearrange("p a t (m j) -> p a t m j", j=J)
+            else:
+                o = xg[b][:].rearrange("p (t m j) -> p m t j", t=J, j=J)[:, m0:m1]
+                i_ = xp[b][:].rearrange("p j (m t) -> p m t j", t=J)[:, m0:m1]
+            eng_copy(e, o, i_)
+
+        def x_part(b, q):
+            x_inter(b, q * P // 4, (q + 1) * P // 4, XE[q])
 
         def quant_x(b):
             if b >= NB:
@@ -266,7 +283,10 @@ def tile_temporalaugmentedbilinear_kernel(tc, x_bytes, x_scale, w1, g, w, w2, la
                 return
             c = i % J
             rec[i] = st.tile([P, 1], F32, name="rec")
-            nc.vector.reciprocal(out=rec[i][:], in_=ssum[i][:])
+            if REC == "V":
+                nc.vector.reciprocal(out=rec[i][:], in_=ssum[i][:])
+            else:
+                nc.gpsimd.tensor_tensor(out=rec[i][:], in0=ssum[i][:], in1=neg1[:], op=ALU.pow)
             if i in pez:
                 dg[i] = st.tile([P, P], F32, name="dg")
                 nc.gpsimd.tensor_scalar(out=dg[i][:], in0=ident[:], scalar1=rec[i][:], scalar2=L[:, c : c + 1], op0=ALU.mult, op1=ALU.mult)
@@ -296,7 +316,7 @@ def tile_temporalaugmentedbilinear_kernel(tc, x_bytes, x_scale, w1, g, w, w2, la
             if i < 0:
                 return
             b, c = divmod(i, J)
-            o = ep.tile([P, N], F32, name="O")
+            o = ep.tile([P, N], F32, name="O", bufs=8)
             src = z_ps[i] if i in pez else Z[i]
             nc.scalar.activation(out=o[:], in_=src[:], func=ACT.Tanh)
             nc.sync.dma_start(out=out[b].rearrange("(m c) q -> m c q", c=J)[:, c, :], in_=o[:])
@@ -320,15 +340,9 @@ def tile_temporalaugmentedbilinear_kernel(tc, x_bytes, x_scale, w1, g, w, w2, la
         deq(0, 2, "V")
         for c in range(4):
             w1_part(c, "S")
-        x_inter(0, 0, "V")
-        x_inter(0, 1, "V")
-        quant_xp(0, 0)
-        x_inter(0, 2, "V")
-        quant_xp(0, 1)
-        x_inter(0, 3, "V")
-        quant_xp(0, 2)
+        x_inter(0, 0, P, "V")
+        quant_x(0)
         quant(wq["w1"][1], wq["w1"][2], wq["w1"][0], 0, P)
-        quant_xp(0, 3)
         mm_hA(0, 0)
         quant(wq["w1"][1], wq["w1"][2], wq["w1"][0], P, 2 * P)
         quant(wq["w1"][1], wq["w1"][2], wq["w1"][0], 2 * P, N)
@@ -337,8 +351,8 @@ def tile_temporalaugmentedbilinear_kernel(tc, x_bytes, x_scale, w1, g, w, w2, la
             w_inter("w", w_sb, WENG[q], 128 * q, 128 * (q + 1))
         for q in range(4):
             w_inter("w2", w2_sb, W2ENG[q], 128 * q, 128 * (q + 1))
-        deq(1, 0, "V")
-        deq(1, 1, "V")
+        deq(1, 0, PD1[0])
+        deq(1, 1, PD1[1])
         evacA(0, 0)
         evacA(0, 1)
         mm_hA(0, 2)
@@ -348,8 +362,8 @@ def tile_temporalaugmentedbilinear_kernel(tc, x_bytes, x_scale, w1, g, w, w2, la
         mm_e(0)
         quant_h(0, 1, 2)
         mm_e(1)
-        deq(1, 2, "V")
-        deq(1, 3, "V")
+        deq(1, 2, PD1[2])
+        deq(1, 3, PD1[3])
         rowmax(0)
         expo(0)
         L = keep.tile([P, J], F32, name="L")
@@ -366,72 +380,78 @@ def tile_temporalaugmentedbilinear_kernel(tc, x_bytes, x_scale, w1, g, w, w2, la
         mm_u(0)
         quant_h(0, 2, 4)
         small(0)
-        for jj in range(J):
-            x_inter(1, jj, PX1[jj])
+        small2(0)
+        if PX == "V":
+            x_inter(1, 0, P, "V")
+        else:
+            for q in range(4):
+                x_inter(1, 32 * q, 32 * (q + 1), PX[q])
         for j in range(J):
             deq(2, j, PD2[j])
-        if PX1 == "VVVV":
-            quant_x(1)
 
         for i in range(NT):
             b, s = divmod(i, J)
             nb = b + 1
             mm_u(i + 1)
             rowmax(i + 1)
-            small2(i)
-            gate(i)
             if s == 0:
-                if b == 0 and PX1 != "VVVV":
-                    quant_x(1)
+                if b > 0:
+                    quant_h(b, 2, 4)
+                mm_e(i + 2)
+                quant_x(nb)
                 mm_hA(nb, 0)
                 if HB:
                     mm_hB(nb, 0)
+                else:
+                    mm_hA(nb, 1)
+            if s == 2:
+                quant_h(nb, 0, 2)
+            if s > 0:
+                mm_e(i + 2)
+            if HB and IBP and s == 3:
+                interB(nb, 0, BINT[0])
+                interB(nb, 1, BINT[1])
+            mix(i - 1)
+            gate(i)
+            if s == 0:
+                evacA(nb, 0)
+                if HB:
+                    mm_hA(nb, 1)
             if s == 1:
-                quant_h(nb, 0, 1)
-                mm_hA(nb, 1)
+                evacA(nb, 1)
                 if HB:
                     mm_hB(nb, 1)
                 else:
                     mm_hA(nb, 2)
             if s == 2:
-                quant_h(nb, 1, 2)
                 if not HB:
+                    evacA(nb, 2)
                     mm_hA(nb, 3)
-                deq(b + 3, 0, "S")
             if s == 3:
-                deq(b + 3, 2, "S")
-            mm_e(i + 2)
-            expo(i + 1)
-            small(i + 1)
-            mix(i - 1)
-            final(i - 2)
-            if s == 0:
-                evacA(nb, 0)
-                if HB:
-                    evacB(nb, 0)
-                    evacB(nb, 1)
-                x_inter(b + 2, 0, XINT[0])
-                x_inter(b + 2, 1, XINT[1])
-            if s == 1:
-                evacA(nb, 1)
-                if HB:
-                    evacB(nb, 2)
-                    evacB(nb, 3)
-                x_inter(b + 2, 2, XINT[2])
-                x_inter(b + 2, 3, XINT[3])
-            if s == 2:
-                deq(b + 3, 1, "V" if DEQV > 0 else "S")
-                if HB:
+                if HB and not IBP:
                     interB(nb, 0, BINT[0])
                     interB(nb, 1, BINT[1])
-                else:
-                    evacA(nb, 2)
-            if s == 3:
                 if not HB:
                     evacA(nb, 3)
-                deq(b + 3, 3, "V" if DEQV > 1 else "S")
-                quant_h(nb, 2, 4)
-                quant_x(b + 2)
+            if s == 0:
+                deq(b + 3, 0, DE[0])
+            if s == 3:
+                deq(b + 3, 2, DE[2])
+            expo(i + 1)
+            final(i - 2)
+            if s == 0:
+                deq(b + 3, 1, DE[1])
+            if s == 3:
+                deq(b + 3, 3, DE[3])
+            if HB and s == 1:
+                evacB(nb, 0)
+                evacB(nb, 1)
+            if HB and s == 2:
+                evacB(nb, 2)
+                evacB(nb, 3)
+            small(i + 1)
+            x_part(b + 2, s)
+            small2(i + 1)
         mix(NT - 1)
         final(NT - 2)
         final(NT - 1)

from contextlib import ExitStack

import concourse.mybir as mybir
from concourse.masks import make_identity

F32 = mybir.dt.float32
BF16 = mybir.dt.bfloat16
U32 = mybir.dt.uint32
U8 = mybir.dt.uint8
FP8 = mybir.dt.float8_e4m3fn
FP8X4 = mybir.dt.float8_e4m3fn_x4
ALU = mybir.AluOpType
ACT = mybir.ActivationFunctionType
AX = mybir.AxisListType

NB, N, P, J = 8, 512, 128, 4
NT = NB * J
FLOPS = 6 * NB * N * N * N
EPS = 1e-12

PEZ = 1
XINT = "VVVV"
HB = 1
DEQV = 0
PD1 = "VVVV"
PX = 'SSVV'
XE = 'SVSV'
DE = "SSSS"
PEX = (6, 14, 22, 26)
PEM = (1, 3)
IBP = 0
PX1 = "VVVV"
RENG = 'G'
REC = 'G'
CENG = 'G'
BINT = 'VV'
WENG = 'SSSS'
W2ENG = 'SSSS'
EB = "SSSS"
PD2 = "SSSS"


def tile_temporalaugmentedbilinear_kernel(tc, x_bytes, x_scale, w1, g, w, w2, lam, bias, out):
    nc = tc.nc
    pez = set(i for i in range(NT - 2) if PEZ and (i % 4 in PEM or i in PEX))
    with ExitStack() as ctx:
        keep = ctx.enter_context(tc.tile_pool(name="keep", bufs=1))
        xpool = ctx.enter_context(tc.tile_pool(name="xpool", bufs=2))
        ep = ctx.enter_context(tc.tile_pool(name="ep", bufs=3))
        st = ctx.enter_context(tc.tile_pool(name="st", bufs=6))
        ps = ctx.enter_context(tc.psum_pool(name="ps", bufs=2))
        hbufs = 2 if PEZ else 4

        ctx.enter_context(tc.manual_schedule())

        xs4 = keep.tile([P, J], F32, name="xs4")
        nc.sync.dma_start(out=xs4[:], in_=x_scale.rearrange("o (p j) e -> p (o j e)", j=J))
        xb = {}

        def load_x(b):
            t = keep.tile([P, J, N], U8, name="xb%d" % b, align_bytes=64)
            xb[b] = t
            nc.sync.dma_start(out=t[:], in_=x_bytes[b].rearrange("(p j) t -> p j t", j=J))

        load_x(0)
        w1_sb = keep.tile([P, J * N], BF16, name="w1_sb", align_bytes=64)
        nc.sync.dma_start(out=w1_sb[:], in_=w1.rearrange("(m c) d -> m (c d)", c=J))
        g_bf = keep.tile([P, J], BF16, name="g_bf")
        nc.sync.dma_start(out=g_bf[:], in_=g.rearrange("(p j) -> p j", j=J))
        w_sb = keep.tile([P, J, N], BF16, name="w_sb", align_bytes=64)
        nc.sync.dma_start(out=w_sb[:], in_=w.rearrange("(p j) q -> p j q", j=J))
        w2_sb = keep.tile([P, J, N], BF16, name="w2_sb", align_bytes=64)
        nc.sync.dma_start(out=w2_sb[:], in_=w2.rearrange("(p j) q -> p j q", j=J))
        load_x(1)
        lam_bf = keep.tile([P, J], BF16, name="lam_bf")
        nc.sync.dma_start(out=lam_bf[:], in_=lam.rearrange("(m c) -> m c", c=J))
        bias_sb = keep.tile([P, J, N], BF16, name="bias_sb", align_bytes=64)
        nc.sync.dma_start(out=bias_sb[:], in_=bias.rearrange("(m c) q -> m c q", c=J))
        for b in range(2, NB):
            load_x(b)

        warm = keep.tile([P, 1], F32, name="warm")
        nc.vector.memset(warm[:], 0.0)
        nc.scalar.activation(out=warm[:], in_=warm[:], func=ACT.Exp)
        ident = keep.tile([P, P], F32, name="ident")
        make_identity(nc, ident[:])
        if PEZ:
            ident_bf = keep.tile([P, P], BF16, name="ident_bf")
            nc.gpsimd.tensor_copy(out=ident_bf[:], in_=ident[:])
        g_f = keep.tile([P, J], F32, name="g_f")
        nc.gpsimd.tensor_copy(out=g_f[:], in_=g_bf[:])

        if REC != "V":
            neg1 = keep.tile([P, 1], F32, name="neg1")
            nc.gpsimd.memset(neg1[:], -1.0)

        wq = {}
        for nm in ("w1", "w", "w2"):
            wq[nm] = (
                keep.tile([P, N * J], BF16, name=nm + "_g", align_bytes=64),
                keep.tile([P, N], U32, name=nm + "_c", align_bytes=64),
                keep.tile([P, N], U8, name=nm + "_s", align_bytes=64),
            )

        def quant(codes, scales, src, lo, hi):
            nc.vector.quantize_mx(out=codes[:, lo:hi].bitcast(FP8X4), scales=scales[:, lo:hi], in_=src[:, J * lo : J * hi])

        def quant_w(nm):
            gr, codes, scales = wq[nm]
            quant(codes, scales, gr, 0, N)

        def eng_copy(e, out, in_):
            if e == "V":
                nc.vector.tensor_copy(out=out, in_=in_)
            elif e == "S":
                nc.scalar.copy(out=out, in_=in_)
            else:
                nc.gpsimd.tensor_scalar(out=out, in0=in_, scalar1=1.0, scalar2=0.0, op0=ALU.mult, op1=ALU.add)

        def w_inter(nm, src, e, lo, hi):
            gr = wq[nm][0]
            eng_copy(
                e,
                gr[:, J * lo : J * hi].rearrange("p (q j) -> p q j", j=J),
                src[:, :, lo:hi].rearrange("p j q -> p q j"),
            )

        xp, xg, xc, xsc = {}, {}, {}, {}

        def deq(b, j, e):
            if b >= NB:
                return
            if b not in xp:
                xp[b] = xpool.tile([P, J, N], BF16, name="xp", bufs=3, align_bytes=64)
            src = xb[b][:, j, :].bitcast(FP8)
            if e == "V":
                nc.vector.tensor_scalar(out=xp[b][:, j, :], in0=src, scalar1=xs4[:, j : j + 1], scalar2=None, op0=ALU.mult)
            else:
                nc.scalar.activation(out=xp[b][:, j, :], in_=src, func=ACT.Copy, scale=xs4[:, j : j + 1])

        def x_inter(b, m0, m1, e):
            if b >= NB:
                return
            if b not in xg:
                xg[b] = xpool.tile([P, N * J], BF16, name="xg", align_bytes=64)
            if e == "V":
                o = xg[b][:].rearrange("p (t a m j) -> p a t (m j)", t=J, a=P // 2, j=J)[:, m0 // 2 : m1 // 2]
                i_ = xp[b][:].rearrange("p j (a m t) -> p a t m j", t=J, m=2)[:, m0 // 2 : m1 // 2]
                o = o.rearrange("p a t (m j) -> p a t m j", j=J)
            else:
                o = xg[b][:].rearrange("p (t m j) -> p m t j", t=J, j=J)[:, m0:m1]
                i_ = xp[b][:].rearrange("p j (m t) -> p m t j", t=J)[:, m0:m1]
            eng_copy(e, o, i_)

        def x_part(b, q):
            x_inter(b, q * P // 4, (q + 1) * P // 4, XE[q])

        def quant_x(b):
            if b >= NB:
                return
            xc[b] = xpool.tile([P, N], U32, name="xc", align_bytes=64)
            xsc[b] = xpool.tile([P, N], U8, name="xsc", align_bytes=64)
            quant(xc[b], xsc[b], xg[b], 0, N)

        def quant_xp(b, jj):
            if b not in xc:
                xc[b] = xpool.tile([P, N], U32, name="xc", align_bytes=64)
                xsc[b] = xpool.tile([P, N], U8, name="xsc", align_bytes=64)
            quant(xc[b], xsc[b], xg[b], jj * P, (jj + 1) * P)

        hg, hc, hs, hp, hpl = {}, {}, {}, {}, {}

        def h_tiles(b):
            if b not in hg:
                hg[b] = xpool.tile([P, N * J], BF16, name="hg", align_bytes=64)
                hc[b] = xpool.tile([P, N], U32, name="hc", align_bytes=64)
                hs[b] = xpool.tile([P, N], U8, name="hs", align_bytes=64)

        def mx(out_ap, lc, ls, rc, rs):
            nc.tensor.matmul_mx(out=out_ap, lhsT=lc.bitcast(FP8X4), lhsT_scale=ls, rhs=rc.bitcast(FP8X4), rhs_scale=rs, start=True, stop=True)

        def mm_hA(b, c):
            if b >= NB:
                return
            t = ps.tile([P, J, P], F32, name="hps", tag="h", bufs=hbufs)
            hp[(b, c)] = t
            wc_, ws_ = wq["w1"][1], wq["w1"][2]
            for jj in range(J):
                s = slice(jj * P, (jj + 1) * P)
                r = slice(c * P, (c + 1) * P)
                mx(t[:, jj, :], xc[b][:, s], xsc[b][:, s], wc_[:, r], ws_[:, r])

        def evacA(b, c):
            if b >= NB:
                return
            h_tiles(b)
            nc.vector.tensor_tensor(
                out=hg[b][:, c * P * J : (c + 1) * P * J].rearrange("p (n j) -> p n j", j=J),
                in0=hp[(b, c)][:].rearrange("p j n -> p n j"),
                in1=g_bf[:].unsqueeze(1).to_broadcast([P, P, J]),
                op=ALU.mult,
            )

        def mm_hB(b, half):
            if b >= NB:
                return
            t = ps.tile([P, 2, 2 * P], F32, name="hpb", tag="h", bufs=hbufs)
            hp[(b, "B", half)] = t
            wc_, ws_ = wq["w1"][1], wq["w1"][2]
            for k in range(2):
                jj = 2 * half + k
                s = slice(jj * P, (jj + 1) * P)
                r = slice(2 * P, 4 * P)
                mx(t[:, k, :], xc[b][:, s], xsc[b][:, s], wc_[:, r], ws_[:, r])

        def evacB(b, jj):
            if b >= NB:
                return
            h_tiles(b)
            if b not in hpl:
                hpl[b] = xpool.tile([P, J, 2 * P], BF16, name="hpl", align_bytes=64)
            nc.scalar.activation(out=hpl[b][:, jj, :], in_=hp[(b, "B", jj // 2)][:, jj % 2, :], func=ACT.Copy, scale=g_f[:, jj : jj + 1])

        def interB(b, part, e):
            if b >= NB:
                return
            a = (2 + part) * P * J
            eng_copy(
                e,
                hg[b][:, a : a + P * J].rearrange("p (n j) -> p n j", j=J),
                hpl[b][:, :, part * P : (part + 1) * P].rearrange("p j n -> p n j"),
            )

        def quant_h(b, lo, hi):
            if b >= NB:
                return
            quant(hc[b], hs[b], hg[b], lo * P, hi * P)

        e_ps, u_ps, z_ps, E, G, Z = {}, {}, {}, {}, {}, {}
        nmax, ssum, rr, rec, cc, dg = {}, {}, {}, {}, {}, {}

        def mm2(i, nm, store, tag):
            if i >= NT:
                return
            b, c = divmod(i, J)
            t = ps.tile([P, N], F32, name=tag + "ps", tag=tag, bufs=2)
            store[i] = t
            s = slice(c * P, (c + 1) * P)
            mx(t[:], hc[b][:, s], hs[b][:, s], wq[nm][1][:], wq[nm][2][:])

        def mm_e(i):
            mm2(i, "w", e_ps, "e")

        def mm_u(i):
            mm2(i, "w2", u_ps, "u")

        def rowmax(i):
            if i >= NT:
                return
            nmax[i] = st.tile([P, 1], F32, name="nmax")
            nc.vector.tensor_reduce(out=nmax[i][:], in_=e_ps[i][:], axis=AX.X, op=ALU.max, negate=True)

        def expo(i):
            if i >= NT:
                return
            E[i] = ep.tile([P, N], F32, name="E")
            ssum[i] = st.tile([P, 1], F32, name="ssum")
            nc.scalar.activation(out=E[i][:], in_=e_ps[i][:], func=ACT.Exp, bias=nmax[i][:], accum_out=ssum[i][:])

        def small(i):
            if i >= NT:
                return
            c = i % J
            rr[i] = st.tile([P, 1], F32, name="rr")
            if RENG == "S":
                nc.scalar.activation(out=rr[i][:], in_=ssum[i][:], func=ACT.Copy, scale=kk[:, c : c + 1])
            else:
                e = nc.gpsimd if RENG == "G" else nc.vector
                e.tensor_tensor(out=rr[i][:], in0=ssum[i][:], in1=kk[:, c : c + 1], op=ALU.mult)

        def small2(i):
            if i >= NT:
                return
            c = i % J
            rec[i] = st.tile([P, 1], F32, name="rec")
            if REC == "V":
                nc.vector.reciprocal(out=rec[i][:], in_=ssum[i][:])
            else:
                nc.gpsimd.tensor_tensor(out=rec[i][:], in0=ssum[i][:], in1=neg1[:], op=ALU.pow)
            if i in pez:
                dg[i] = st.tile([P, P], F32, name="dg")
                nc.gpsimd.tensor_scalar(out=dg[i][:], in0=ident[:], scalar1=rec[i][:], scalar2=L[:, c : c + 1], op0=ALU.mult, op1=ALU.mult)
            else:
                cc[i] = st.tile([P, 1], F32, name="cc")
                e = nc.gpsimd if CENG == "G" else nc.vector
                e.tensor_tensor(out=cc[i][:], in0=rec[i][:], in1=L[:, c : c + 1], op=ALU.mult)

        def gate(i):
            G[i] = ep.tile([P, N], F32, name="G")
            nc.vector.scalar_tensor_tensor(out=G[i][:], in0=E[i][:], scalar=rr[i][:], in1=u_ps[i][:], op0=ALU.add, op1=ALU.mult)

        def mix(i):
            if i < 0:
                return
            c = i % J
            if i in pez:
                t = ps.tile([P, N], F32, name="zps", tag="z", bufs=2)
                z_ps[i] = t
                nc.tensor.matmul(t[:], lhsT=ident_bf[:], rhs=bias_sb[:, c, :], start=True, stop=False)
                nc.tensor.matmul(t[:], lhsT=dg[i][:], rhs=G[i][:], start=False, stop=True)
            else:
                Z[i] = ep.tile([P, N], F32, name="Z")
                nc.vector.scalar_tensor_tensor(out=Z[i][:], in0=G[i][:], scalar=cc[i][:], in1=bias_sb[:, c, :], op0=ALU.mult, op1=ALU.add)

        def final(i):
            if i < 0:
                return
            b, c = divmod(i, J)
            o = ep.tile([P, N], F32, name="O", bufs=8)
            src = z_ps[i] if i in pez else Z[i]
            nc.scalar.activation(out=o[:], in_=src[:], func=ACT.Tanh)
            nc.sync.dma_start(out=out[b].rearrange("(m c) q -> m c q", c=J)[:, c, :], in_=o[:])

        def w1_part(c, e):
            t = ps.tile([P, 2, P], F32, name="w1t", tag="h", bufs=hbufs)
            for u in range(2):
                nc.tensor.transpose(t[:, u, :], words[:, 256 * c + u : 256 * (c + 1) : 2], ident[:])
            o = w1g_words[:, 256 * c : 256 * (c + 1)].rearrange("p (m u) -> p m u", u=2)
            i_ = t[:].rearrange("p u m -> p m u")
            if e == "S":
                nc.scalar.copy(out=o, in_=i_)
            else:
                nc.vector.tensor_copy(out=o, in_=i_)

        words = w1_sb[:].bitcast(F32)
        w1g_words = wq["w1"][0][:].bitcast(F32)
        deq(0, 0, "V")
        deq(0, 3, "S")
        deq(0, 1, "V")
        deq(0, 2, "V")
        for c in range(4):
            w1_part(c, "S")
        x_inter(0, 0, P, "V")
        quant_x(0)
        quant(wq["w1"][1], wq["w1"][2], wq["w1"][0], 0, P)
        mm_hA(0, 0)
        quant(wq["w1"][1], wq["w1"][2], wq["w1"][0], P, 2 * P)
        quant(wq["w1"][1], wq["w1"][2], wq["w1"][0], 2 * P, N)
        mm_hA(0, 1)
        for q in range(4):
            w_inter("w", w_sb, WENG[q], 128 * q, 128 * (q + 1))
        for q in range(4):
            w_inter("w2", w2_sb, W2ENG[q], 128 * q, 128 * (q + 1))
        deq(1, 0, PD1[0])
        deq(1, 1, PD1[1])
        evacA(0, 0)
        evacA(0, 1)
        mm_hA(0, 2)
        mm_hA(0, 3)
        quant_w("w")
        quant_h(0, 0, 1)
        mm_e(0)
        quant_h(0, 1, 2)
        mm_e(1)
        deq(1, 2, PD1[2])
        deq(1, 3, PD1[3])
        rowmax(0)
        expo(0)
        L = keep.tile([P, J], F32, name="L")
        nc.vector.tensor_scalar(out=L[:], in0=lam_bf[:], scalar1=float(N), scalar2=EPS, op0=ALU.mult, op1=ALU.add)
        rl = keep.tile([P, J], F32, name="rl")
        nc.vector.reciprocal(out=rl[:], in_=L[:])
        dd = keep.tile([P, J], F32, name="dd")
        nc.gpsimd.tensor_scalar(out=dd[:], in0=lam_bf[:], scalar1=-1.0, scalar2=1.0, op0=ALU.mult, op1=ALU.add)
        kk = keep.tile([P, J], F32, name="kk")
        nc.gpsimd.tensor_tensor(out=kk[:], in0=dd[:], in1=rl[:], op=ALU.mult)
        evacA(0, 2)
        evacA(0, 3)
        quant_w("w2")
        mm_u(0)
        quant_h(0, 2, 4)
        small(0)
        small2(0)
        if PX == "V":
            x_inter(1, 0, P, "V")
        else:
            for q in range(4):
                x_inter(1, 32 * q, 32 * (q + 1), PX[q])
        for j in range(J):
            deq(2, j, PD2[j])

        for i in range(NT):
            b, s = divmod(i, J)
            nb = b + 1
            mm_u(i + 1)
            rowmax(i + 1)
            if s == 0:
                if b > 0:
                    quant_h(b, 2, 4)
                mm_e(i + 2)
                quant_x(nb)
                mm_hA(nb, 0)
                if HB:
                    mm_hB(nb, 0)
                else:
                    mm_hA(nb, 1)
            if s == 2:
                quant_h(nb, 0, 2)
            if s > 0:
                mm_e(i + 2)
            if HB and IBP and s == 3:
                interB(nb, 0, BINT[0])
                interB(nb, 1, BINT[1])
            mix(i - 1)
            gate(i)
            if s == 0:
                evacA(nb, 0)
                if HB:
                    mm_hA(nb, 1)
            if s == 1:
                evacA(nb, 1)
                if HB:
                    mm_hB(nb, 1)
                else:
                    mm_hA(nb, 2)
            if s == 2:
                if not HB:
                    evacA(nb, 2)
                    mm_hA(nb, 3)
            if s == 3:
                if HB and not IBP:
                    interB(nb, 0, BINT[0])
                    interB(nb, 1, BINT[1])
                if not HB:
                    evacA(nb, 3)
            if s == 0:
                deq(b + 3, 0, DE[0])
            if s == 3:
                deq(b + 3, 2, DE[2])
            expo(i + 1)
            final(i - 2)
            if s == 0:
                deq(b + 3, 1, DE[1])
            if s == 3:
                deq(b + 3, 3, DE[3])
            if HB and s == 1:
                evacB(nb, 0)
                evacB(nb, 1)
            if HB and s == 2:
                evacB(nb, 2)
                evacB(nb, 3)
            small(i + 1)
            x_part(b + 2, s)
            small2(i + 1)
        mix(NT - 1)
        final(NT - 2)
        final(NT - 1)
